import numpy as np
import ml_dtypes


def mxq(x, axis, fmt="e4m3"):
    dtype, down = {"e4m3": (ml_dtypes.float8_e4m3fn, 7), "e5m2": (ml_dtypes.float8_e5m2, 14)}[fmt]
    v = np.moveaxis(np.asarray(x, np.float32).astype(ml_dtypes.bfloat16).astype(np.float64), axis, -1)
    blocks = v.reshape(v.shape[:-1] + (-1, 32))
    amax = np.abs(blocks).max(-1, keepdims=True)
    byte = np.maximum(np.where(amax > 0, np.frexp(amax)[1] - 1 + 127, 0) - down, 1)
    scale = np.exp2(byte - 127.0)
    codes = (blocks / scale).astype(np.float32).astype(dtype).astype(np.float64)
    return np.moveaxis((codes * scale).reshape(v.shape), -1, axis)


WIDE = False


def mx_kscale(k):
    if not WIDE:
        return np.ones(k)
    levels = np.array([10, -10, 5, -5, 0])
    if k % 512:
        return np.exp2(np.random.permutation(np.resize(levels, k // 32))).repeat(32)
    a = np.empty((k // 512, 16))
    for p in range(k // 512):
        a[p, :8] = np.random.permutation(np.resize(levels, 8))
        for g in range(8):
            far = levels[np.abs(levels - a[p, g]) >= 10]
            a[p, g + 8] = far[np.random.randint(len(far))]
    return np.exp2(a.ravel()).repeat(32)


def f64(x):
    return np.asarray(x).astype(np.float64)


def striped(idx):
    return np.tile(idx.reshape(-1, 16).T, (8, 1)).astype(np.uint16)


def unstriped(offs):
    return offs[:16].T.reshape(-1).astype(np.int64)


def pack_weight(w):
    k, n = w.shape
    w = f64(np.asarray(w, np.float32).astype(ml_dtypes.bfloat16)).reshape(k // 32, 32, n)
    amax = np.abs(w).max(1)
    byte = np.clip(np.where(amax > 0, np.frexp(amax)[1] - 1 + 127 - 7, 1), 1, 254)
    scaled = (w * np.exp2(127.0 - byte)[:, None, :]).reshape(k, n).astype(np.float32)
    words = np.ascontiguousarray(scaled.reshape(k // 512, 128, 4, n).transpose(0, 1, 3, 2)).astype(ml_dtypes.float8_e4m3fn).view(np.uint8)
    return words, np.ascontiguousarray(byte.astype(np.uint8).reshape(k // 512, 16, n))


def unpack_weight(words, scales):
    g, p, n, _ = words.shape
    vals = np.ascontiguousarray(words).view(ml_dtypes.float8_e4m3fn).astype(np.float64) * np.repeat(np.exp2(scales.astype(np.float64) - 127.0), 8, axis=1)[..., None]
    return vals.transpose(0, 1, 3, 2).reshape(g * 512, n)


def gelu(v):
    return 0.5 * v * (1.0 + np.tanh(np.sqrt(2.0 / np.pi) * (v + 0.044715 * v**3)))


K, T, S, N = 512, 1024, 512, 128


def setup_inputs():
    n = np.random.standard_normal
    s = mx_kscale(K)[:, None]
    words, scales = pack_weight(n((K, N)) / np.sqrt(K) / s)
    return {
        "xT": (n((K, S)) * s).astype(np.float32),
        "w_words": words,
        "w_scales": scales,
        "b": (0.3 * n((N, 1))).astype(np.float32),
        "gate": np.tile(np.random.uniform(0.2, 1.0, S), (N, 1)).astype(np.float32),
        "offs": striped(np.random.permutation(T)[:S]),
    }


def reference(xT, w_words, w_scales, b, gate, offs):
    w = unpack_weight(w_words, w_scales)
    idx = unstriped(offs)
    xq = mxq(f64(xT), 0, "e4m3")
    y = w.T @ xq
    y = gelu(y + f64(b))
    out = np.zeros((N, T))
    out[:, idx] = f64(gate) * y
    return out

@@ -1,0 +1,118 @@
+from contextlib import ExitStack
+
+import concourse.mybir as mybir
+
+K, S, T, N = 512, 512, 1024, 128
+FLOPS = 2 * K * S * N
+
+F32 = mybir.dt.float32
+BF16 = mybir.dt.bfloat16
+I32 = mybir.dt.int32
+U32 = mybir.dt.uint32
+U16 = mybir.dt.uint16
+U8 = mybir.dt.uint8
+FP8X4 = mybir.dt.float8_e4m3fn_x4
+GELU = mybir.ActivationFunctionType.Gelu_apprx_tanh
+MULT = mybir.AluOpType.mult
+
+P = 128
+PACK = 4
+PIECE = 128
+LOADS = ((0, 128), (128, 256), (256, 512))
+
+
+def tile_picked_place_lin_gelu_sub_l_kernel(tc, xT, w_words, w_scales, b, gate, offs, out):
+    nc = tc.nc
+    with ExitStack() as ctx:
+        keep = ctx.enter_context(tc.tile_pool(name="keep", bufs=1))
+        psum = ctx.enter_context(tc.psum_pool(name="psum", bufs=1))
+
+        offsets = keep.tile([P, S // 16], U16, name="offsets")
+        w_codes = keep.tile([P, N], U32, name="w_codes", align_bytes=64)
+        w_plane = keep.tile([P, N], U8, name="w_plane", align_bytes=64)
+        bias = keep.tile([P, 1], F32, name="bias")
+        gates = keep.tile([P, S], F32, name="gates", align_bytes=64)
+        window = keep.tile([P, T], F32, name="window", align_bytes=64)
+        warm_in = keep.tile([P, 1], F32, name="warm_in")
+        warm_out = keep.tile([P, 1], F32, name="warm_out")
+
+        x_rows = xT.rearrange("(p j) w -> p j w", j=PACK)
+        raw = []
+        for lo, hi in LOADS:
+            t = keep.tile([P, PACK, hi - lo], F32, name=f"raw{lo}", align_bytes=64)
+            nc.sync.dma_start(out=t[:], in_=x_rows[:, :, lo:hi])
+            raw.append((lo, hi, t))
+        nc.sync.dma_start(offsets[:], offs)
+
+        nc.vector.memset(w_plane[:].bitcast(I32), 0)
+        nc.vector.memset(warm_in[:], 0.0)
+        nc.scalar.dma_start(out=w_codes[:].bitcast(I32), in_=w_words[0].rearrange("p n t -> p (n t)").bitcast(I32))
+        for q in range(4):
+            nc.scalar.dma_start(
+                out=w_plane[32 * q : 32 * q + 4, :].bitcast(I32),
+                in_=w_scales[0, 4 * q : 4 * q + 4, :].bitcast(I32),
+            )
+        nc.gpsimd.dma_start(out=bias[:], in_=b)
+        nc.gpsimd.dma_start(out=gates[:], in_=gate)
+        nc.scalar.activation(warm_out[:], warm_in[:], GELU)
+        nc.vector.memset(window[:], 0.0)
+
+        grouped, codes, planes, acc, y = [], [], [], [], []
+        for i in range(S // PIECE):
+            grouped.append(keep.tile([P, PIECE, PACK], BF16, name=f"grouped{i}", align_bytes=64))
+            codes.append(keep.tile([P, PIECE], U32, name=f"codes{i}", align_bytes=64))
+            planes.append(keep.tile([P, PIECE], U8, name=f"planes{i}", align_bytes=64))
+            acc.append(psum.tile([N, PIECE], F32, name=f"acc{i}"))
+            y.append(keep.tile([N, PIECE], F32, name=f"y{i}", align_bytes=64))
+
+        def interleave(i, copy):
+            for lo, hi, t in raw:
+                if lo <= i * PIECE < hi:
+                    cols = slice(i * PIECE - lo, (i + 1) * PIECE - lo)
+                    copy(out=grouped[i][:], in_=t[:, :, cols].rearrange("p j w -> p w j"))
+
+        def quantise(i):
+            nc.vector.quantize_mx(
+                out=codes[i][:].bitcast(FP8X4),
+                scales=planes[i][:],
+                in_=grouped[i][:].rearrange("p w j -> p (w j)"),
+            )
+
+        def multiply(i):
+            nc.tensor.matmul_mx(
+                out=acc[i][:],
+                lhsT=w_codes[:].bitcast(FP8X4),
+                lhsT_scale=w_plane[:],
+                rhs=codes[i][:].bitcast(FP8X4),
+                rhs_scale=planes[i][:],
+                start=True,
+                stop=True,
+            )
+            nc.scalar.activation(y[i][:], acc[i][:], GELU, bias=bias[:])
+
+        def place(i):
+            cols = slice(i * PIECE // 16, (i + 1) * PIECE // 16)
+            nc.vector.tensor_tensor(
+                window[:].indirect(offsets[:, cols]),
+                y[i][:],
+                gates[:, i * PIECE : (i + 1) * PIECE],
+                MULT,
+            )
+
+        interleave(0, nc.vector.tensor_copy)
+        quantise(0)
+        multiply(0)
+        interleave(1, nc.vector.tensor_copy)
+        quantise(1)
+        multiply(1)
+        interleave(2, nc.scalar.copy)
+        place(0)
+        quantise(2)
+        multiply(2)
+        interleave(3, nc.scalar.copy)
+        place(1)
+        quantise(3)
+        multiply(3)
+        place(2)
+        place(3)
+        nc.sync.dma_start(out=out, in_=window[:])

@@ -18,7 +18,7 @@ MULT = mybir.AluOpType.mult
 P = 128
 PACK = 4
 PIECE = 128
-LOADS = ((0, 128), (128, 256), (256, 512))
+LOADS = ((0, 256), (256, 512))
 
 
 def tile_picked_place_lin_gelu_sub_l_kernel(tc, xT, w_words, w_scales, b, gate, offs, out):
@@ -40,20 +40,29 @@ def tile_picked_place_lin_gelu_sub_l_kernel(tc, xT, w_words, w_scales, b, gate, 
         raw = []
         for lo, hi in LOADS:
             t = keep.tile([P, PACK, hi - lo], F32, name=f"raw{lo}", align_bytes=64)
-            nc.sync.dma_start(out=t[:], in_=x_rows[:, :, lo:hi])
             raw.append((lo, hi, t))
-        nc.sync.dma_start(offsets[:], offs)
 
-        nc.vector.memset(w_plane[:].bitcast(I32), 0)
-        nc.vector.memset(warm_in[:], 0.0)
-        nc.scalar.dma_start(out=w_codes[:].bitcast(I32), in_=w_words[0].rearrange("p n t -> p (n t)").bitcast(I32))
-        for q in range(4):
-            nc.scalar.dma_start(
+        def load(queue, k):
+            lo, hi, t = raw[k]
+            queue.dma_start(out=t[:], in_=x_rows[:, :, lo:hi])
+
+        def load_scales(queue, q):
+            queue.dma_start(
                 out=w_plane[32 * q : 32 * q + 4, :].bitcast(I32),
                 in_=w_scales[0, 4 * q : 4 * q + 4, :].bitcast(I32),
             )
-        nc.gpsimd.dma_start(out=bias[:], in_=b)
+
+        load_scales(nc.sync, 0)
+        load_scales(nc.scalar, 1)
+        load(nc.sync, 0)
+        nc.scalar.dma_start(out=w_codes[:].bitcast(I32), in_=w_words[0].rearrange("p n t -> p (n t)").bitcast(I32))
+        load_scales(nc.sync, 2)
+        nc.scalar.dma_start(out=bias[:], in_=b)
+        load_scales(nc.sync, 3)
         nc.gpsimd.dma_start(out=gates[:], in_=gate)
+        load(nc.sync, 1)
+        nc.sync.dma_start(offsets[:], offs)
+        nc.vector.memset(warm_in[:], 0.0)
         nc.scalar.activation(warm_out[:], warm_in[:], GELU)
         nc.vector.memset(window[:], 0.0)
 
@@ -102,7 +111,7 @@ def tile_picked_place_lin_gelu_sub_l_kernel(tc, xT, w_words, w_scales, b, gate, 
         interleave(0, nc.vector.tensor_copy)
         quantise(0)
         multiply(0)
-        interleave(1, nc.vector.tensor_copy)
+        interleave(1, nc.scalar.copy)
         quantise(1)
         multiply(1)
         interleave(2, nc.scalar.copy)

from contextlib import ExitStack

import concourse.mybir as mybir

K, S, T, N = 512, 512, 1024, 128
FLOPS = 2 * K * S * N

F32 = mybir.dt.float32
BF16 = mybir.dt.bfloat16
I32 = mybir.dt.int32
U32 = mybir.dt.uint32
U16 = mybir.dt.uint16
U8 = mybir.dt.uint8
FP8X4 = mybir.dt.float8_e4m3fn_x4
GELU = mybir.ActivationFunctionType.Gelu_apprx_tanh
MULT = mybir.AluOpType.mult

P = 128
PACK = 4
PIECE = 128
LOADS = ((0, 256), (256, 512))


def tile_picked_place_lin_gelu_sub_l_kernel(tc, xT, w_words, w_scales, b, gate, offs, out):
    nc = tc.nc
    with ExitStack() as ctx:
        keep = ctx.enter_context(tc.tile_pool(name="keep", bufs=1))
        psum = ctx.enter_context(tc.psum_pool(name="psum", bufs=1))

        offsets = keep.tile([P, S // 16], U16, name="offsets")
        w_codes = keep.tile([P, N], U32, name="w_codes", align_bytes=64)
        w_plane = keep.tile([P, N], U8, name="w_plane", align_bytes=64)
        bias = keep.tile([P, 1], F32, name="bias")
        gates = keep.tile([P, S], F32, name="gates", align_bytes=64)
        window = keep.tile([P, T], F32, name="window", align_bytes=64)
        warm_in = keep.tile([P, 1], F32, name="warm_in")
        warm_out = keep.tile([P, 1], F32, name="warm_out")

        x_rows = xT.rearrange("(p j) w -> p j w", j=PACK)
        raw = []
        for lo, hi in LOADS:
            t = keep.tile([P, PACK, hi - lo], F32, name=f"raw{lo}", align_bytes=64)
            raw.append((lo, hi, t))

        def load(queue, k):
            lo, hi, t = raw[k]
            queue.dma_start(out=t[:], in_=x_rows[:, :, lo:hi])

        def load_scales(queue, q):
            queue.dma_start(
                out=w_plane[32 * q : 32 * q + 4, :].bitcast(I32),
                in_=w_scales[0, 4 * q : 4 * q + 4, :].bitcast(I32),
            )

        load_scales(nc.sync, 0)
        load_scales(nc.scalar, 1)
        load(nc.sync, 0)
        nc.scalar.dma_start(out=w_codes[:].bitcast(I32), in_=w_words[0].rearrange("p n t -> p (n t)").bitcast(I32))
        load_scales(nc.sync, 2)
        nc.scalar.dma_start(out=bias[:], in_=b)
        load_scales(nc.sync, 3)
        nc.gpsimd.dma_start(out=gates[:], in_=gate)
        load(nc.sync, 1)
        nc.sync.dma_start(offsets[:], offs)
        nc.vector.memset(warm_in[:], 0.0)
        nc.scalar.activation(warm_out[:], warm_in[:], GELU)
        nc.vector.memset(window[:], 0.0)

        grouped, codes, planes, acc, y = [], [], [], [], []
        for i in range(S // PIECE):
            grouped.append(keep.tile([P, PIECE, PACK], BF16, name=f"grouped{i}", align_bytes=64))
            codes.append(keep.tile([P, PIECE], U32, name=f"codes{i}", align_bytes=64))
            planes.append(keep.tile([P, PIECE], U8, name=f"planes{i}", align_bytes=64))
            acc.append(psum.tile([N, PIECE], F32, name=f"acc{i}"))
            y.append(keep.tile([N, PIECE], F32, name=f"y{i}", align_bytes=64))

        def interleave(i, copy):
            for lo, hi, t in raw:
                if lo <= i * PIECE < hi:
                    cols = slice(i * PIECE - lo, (i + 1) * PIECE - lo)
                    copy(out=grouped[i][:], in_=t[:, :, cols].rearrange("p j w -> p w j"))

        def quantise(i):
            nc.vector.quantize_mx(
                out=codes[i][:].bitcast(FP8X4),
                scales=planes[i][:],
                in_=grouped[i][:].rearrange("p w j -> p (w j)"),
            )

        def multiply(i):
            nc.tensor.matmul_mx(
                out=acc[i][:],
                lhsT=w_codes[:].bitcast(FP8X4),
                lhsT_scale=w_plane[:],
                rhs=codes[i][:].bitcast(FP8X4),
                rhs_scale=planes[i][:],
                start=True,
                stop=True,
            )
            nc.scalar.activation(y[i][:], acc[i][:], GELU, bias=bias[:])

        def place(i):
            cols = slice(i * PIECE // 16, (i + 1) * PIECE // 16)
            nc.vector.tensor_tensor(
                window[:].indirect(offsets[:, cols]),
                y[i][:],
                gates[:, i * PIECE : (i + 1) * PIECE],
                MULT,
            )

        interleave(0, nc.vector.tensor_copy)
        quantise(0)
        multiply(0)
        interleave(1, nc.scalar.copy)
        quantise(1)
        multiply(1)
        interleave(2, nc.scalar.copy)
        place(0)
        quantise(2)
        multiply(2)
        interleave(3, nc.scalar.copy)
        place(1)
        quantise(3)
        multiply(3)
        place(2)
        place(3)
        nc.sync.dma_start(out=out, in_=window[:])
